import numpy as np
import ml_dtypes


def mxq(x, axis, fmt="e4m3"):
    dtype, down = {"e4m3": (ml_dtypes.float8_e4m3fn, 7), "e5m2": (ml_dtypes.float8_e5m2, 14)}[fmt]
    v = np.moveaxis(np.asarray(x, np.float32).astype(ml_dtypes.bfloat16).astype(np.float64), axis, -1)
    blocks = v.reshape(v.shape[:-1] + (-1, 32))
    amax = np.abs(blocks).max(-1, keepdims=True)
    byte = np.maximum(np.where(amax > 0, np.frexp(amax)[1] - 1 + 127, 0) - down, 1)
    scale = np.exp2(byte - 127.0)
    codes = (blocks / scale).astype(np.float32).astype(dtype).astype(np.float64)
    return np.moveaxis((codes * scale).reshape(v.shape), -1, axis)


WIDE = False


def mx_kscale(k):
    if not WIDE:
        return np.ones(k)
    levels = np.array([10, -10, 5, -5, 0])
    if k % 512:
        return np.exp2(np.random.permutation(np.resize(levels, k // 32))).repeat(32)
    a = np.empty((k // 512, 16))
    for p in range(k // 512):
        a[p, :8] = np.random.permutation(np.resize(levels, 8))
        for g in range(8):
            far = levels[np.abs(levels - a[p, g]) >= 10]
            a[p, g + 8] = far[np.random.randint(len(far))]
    return np.exp2(a.ravel()).repeat(32)


def f64(x):
    return np.asarray(x).astype(np.float64)


def striped(idx):
    return np.tile(np.asarray(idx).reshape(-1, 16).T, (8, 1)).astype(np.uint16)


def unstriped(offs):
    return offs[:16].T.reshape(-1).astype(np.int64)


E2M1 = np.array([0.0, 0.5, 1.0, 1.5, 2.0, 3.0, 4.0, 6.0, -0.0, -0.5, -1.0, -1.5, -2.0, -3.0, -4.0, -6.0])


def pack_weight(w, fmt):
    k, n = w.shape
    w = f64(np.asarray(w, np.float32).astype(ml_dtypes.bfloat16)).reshape(k // 32, 32, n)
    amax = np.abs(w).max(1)
    if fmt == "e4m3":
        byte = np.frexp(amax)[1] - 1 + 127 - 7
    else:
        mant, ex = np.frexp(amax / 6.0)
        byte = np.where(mant > 0.5, ex, ex - 1) + 127
    byte = np.clip(np.where(amax > 0, byte, 1), 1, 254)
    scaled = (w * np.exp2(127.0 - byte)[:, None, :]).reshape(k, n).astype(np.float32)
    by_word = np.ascontiguousarray(scaled.reshape(k // 512, 128, 4, n).transpose(0, 1, 3, 2))
    if fmt == "e4m3":
        words = by_word.astype(ml_dtypes.float8_e4m3fn).view(np.uint8)
    else:
        c = by_word.astype(ml_dtypes.float4_e2m1fn).view(np.uint8) & 0xF
        words = (c[..., 0::2] | (c[..., 1::2] << 4)).reshape(k // 512, 128, 2 * n)
    return np.ascontiguousarray(words), np.ascontiguousarray(byte.astype(np.uint8).reshape(k // 512, 16, n))


def unpack_weight(words, scales, fmt):
    g, _, n = scales.shape
    words = np.ascontiguousarray(words).reshape(g, 128, n, -1)
    if fmt == "e4m3":
        vals = words.view(ml_dtypes.float8_e4m3fn).astype(np.float64)
    else:
        nib = np.empty((g, 128, n, 4), np.uint8)
        nib[..., 0::2] = words & 0xF
        nib[..., 1::2] = words >> 4
        vals = E2M1[nib]
    vals = vals * np.repeat(np.exp2(scales.astype(np.float64) - 127.0), 8, axis=1)[..., None]
    return vals.transpose(0, 1, 3, 2).reshape(g * 512, n)


def gelu(v):
    return 0.5 * v * (1.0 + np.tanh(0.7978845608028654 * (v + 0.044715 * v ** 3)))


def bf(x):
    return np.asarray(x, np.float32).astype(ml_dtypes.bfloat16)


def planes(Y):
    r, m = Y.shape
    b = f64(bf(Y)).reshape(r // 32, 32, m)
    amax = np.abs(b).max(1)
    byte = np.clip(np.where(amax > 0, np.frexp(amax)[1] - 1 + 127 - 7, 1), 1, 254)
    codes = (b * np.exp2(127.0 - byte)[:, None, :]).reshape(r, m).astype(np.float32).astype(ml_dtypes.float8_e4m3fn).view(np.uint8)
    words = codes.reshape(r // 512, 128, 4, m).transpose(0, 1, 3, 2)
    return np.ascontiguousarray(words), np.ascontiguousarray(byte.astype(np.uint8).reshape(r // 512, 16, m))


B, N, T, D, NQ = 1, 512, 2048, 512, 256


def setup_inputs():
    n = np.random.standard_normal
    idx = np.random.permutation(T)[:B * N]
    s = mx_kscale(D)[:, None]
    kp = pack_weight(n((D, T)) / s, "e4m3")
    return {
        "qT": (n((B, D, NQ)) * s * (1.00 / np.sqrt(D))).astype(np.float32),
        "k_words": kp[0],
        "k_scales": kp[1],
        "nb": np.tile(0.5 * n(2048), (128, 1)).astype(np.float32),
        "offs": striped(idx),
    }


def reference(qT, k_words, k_scales, nb, offs):
    idx = unstriped(offs)
    pick = lambda x, which: x[:, which].reshape(x.shape[0], B, -1).transpose(1, 0, 2)
    k = unpack_weight(k_words, k_scales, "e4m3")
    kg = pick(k, idx)
    qq = mxq(f64(qT), 1, "e4m3")
    a = kg.transpose(0, 2, 1) @ qq
    y = gelu(a + pick(f64(nb), idx)[:, :1, :].transpose(0, 2, 1))
    Y = y[0]
    words, scales = planes(Y)
    return Y, words, scales

@@ -1,0 +1,138 @@
+from contextlib import ExitStack
+
+import concourse.mybir as mybir
+from concourse.masks import make_identity
+
+F32 = mybir.dt.float32
+BF16 = mybir.dt.bfloat16
+I32 = mybir.dt.int32
+U32 = mybir.dt.uint32
+U16 = mybir.dt.uint16
+U8 = mybir.dt.uint8
+FP8X4 = mybir.dt.float8_e4m3fn_x4
+GELU = mybir.ActivationFunctionType.Gelu_apprx_tanh
+
+P = 128
+PACK = 4
+SLOTS = 512
+POOL = 2048
+NQ = 256
+HALF = 128
+QUADS = 4
+BIAS_ROW = P - 1
+
+FLOPS = 2 * SLOTS * 512 * NQ
+
+
+def tile_attend_plh_bgelu_topk_kernel(tc, qT, k_words, k_scales, nb, offs, out_0, out_1, out_2):
+    nc = tc.nc
+    with ExitStack() as ctx:
+        held = ctx.enter_context(tc.tile_pool(name="held", bufs=1))
+        psum = ctx.enter_context(tc.psum_pool(name="psum", bufs=1))
+
+        offsets = held.tile([P, SLOTS // 16], U16, name="offsets")
+        nc.sync.dma_start(offsets[:], offs)
+
+        scale_pool = held.tile([P, POOL], U8, name="scale_pool", align_bytes=64)
+        nc.vector.memset(scale_pool[:].bitcast(I32), 0)
+        warm_in = held.tile([P, 1], F32, name="warm_in")
+        nc.vector.memset(warm_in[:], 0.0)
+        bias_pool = held.tile([P, POOL], F32, name="bias_pool")
+        nc.vector.memset(bias_pool[0:BIAS_ROW, :], 0.0)
+        nc.sync.dma_start(bias_pool[BIAS_ROW:P, :], nb[0:1, :])
+        for quad in range(QUADS):
+            nc.scalar.dma_start(
+                scale_pool[32 * quad : 32 * quad + 4, :].bitcast(I32),
+                k_scales[0, 4 * quad : 4 * quad + 4, :].bitcast(I32),
+            )
+        warm_out = held.tile([P, 1], F32, name="warm_out")
+        nc.scalar.activation(warm_out[:], warm_in[:], GELU)
+
+        word_pool = held.tile([P, POOL], I32, name="word_pool")
+        nc.sync.dma_start(word_pool[:], k_words[0].rearrange("p n t -> p (n t)").bitcast(I32))
+        q_raw = held.tile([P, PACK, NQ], F32, name="q_raw")
+        nc.sync.dma_start(q_raw[:], qT[0].rearrange("(p j) q -> p j q", j=PACK))
+
+        ident = held.tile([P, P], F32, name="ident")
+        make_identity(nc, ident[:])
+
+        bias_listed = held.tile([P, SLOTS], F32, name="bias_listed")
+        nc.vector.tensor_copy(bias_listed[:], bias_pool[:].indirect(offsets[:]))
+        scale_listed = held.tile([P, SLOTS], U8, name="scale_listed", align_bytes=64)
+        nc.vector.tensor_copy(scale_listed[:], scale_pool[:].indirect(offsets[:]))
+        word_listed = held.tile([P, SLOTS], I32, name="word_listed", align_bytes=64)
+        nc.vector.tensor_copy(word_listed[:].bitcast(U32), word_pool[:].bitcast(U32).indirect(offsets[:]))
+
+        bias_turned = psum.tile([P, PACK, P], F32, name="bias_turned", tag="bank7")
+        for r in range(PACK):
+            nc.tensor.transpose(bias_turned[:, r, :], bias_listed[:, r:SLOTS:PACK], ident[:])
+        bias_cols = held.tile([P, PACK], F32, name="bias_cols")
+        nc.scalar.copy(bias_cols[:], bias_turned[:, :, BIAS_ROW])
+
+        k_scale = held.tile([P, SLOTS], U8, name="k_scale", align_bytes=64)
+        nc.vector.tensor_copy(
+            k_scale[:].rearrange("p (r c i) -> p c r i", r=PACK, i=16),
+            scale_listed[:].rearrange("p (c i r) -> p c r i", r=PACK, i=16),
+        )
+        k_code = held.tile([P, SLOTS], I32, name="k_code", align_bytes=64)
+        nc.vector.tensor_copy(
+            k_code[:].rearrange("p (r c i) -> p c r i", r=PACK, i=4),
+            word_listed[:].rearrange("p (c i r) -> p c r i", r=PACK, i=4),
+        )
+
+        y_scale = held.tile([P, NQ], U8, name="y_scale", align_bytes=64)
+        y_rows = out_0.rearrange("(p r) q -> p r q", r=PACK)
+        y_words = out_1[0].rearrange("p q u -> p (q u)").bitcast(I32)
+
+        q_codes = []
+        q_scales = []
+        for h in range(NQ // HALF):
+            cols = slice(h * HALF, (h + 1) * HALF)
+            q_woven = held.tile([P, HALF, PACK], BF16, name="q_woven%d" % h, align_bytes=64)
+            nc.scalar.copy(
+                q_woven[:].rearrange("p (c i) j -> p c j i", i=4),
+                q_raw[:, :, cols].rearrange("p j (c i) -> p c j i", i=4),
+            )
+            q_code = held.tile([P, HALF], U32, name="q_code%d" % h, align_bytes=64)
+            q_scale = held.tile([P, HALF], U8, name="q_scale%d" % h, align_bytes=64)
+            nc.vector.quantize_mx(
+                out=q_code[:].bitcast(FP8X4), scales=q_scale[:], in_=q_woven[:].rearrange("p c j -> p (c j)")
+            )
+            q_codes.append(q_code)
+            q_scales.append(q_scale)
+
+        for h in range(NQ // HALF):
+            cols = slice(h * HALF, (h + 1) * HALF)
+            y = held.tile([P, PACK, HALF], F32, name="y%d" % h)
+            for r in range(PACK):
+                part = slice(r * P, (r + 1) * P)
+                acc = psum.tile([P, HALF], F32, name="acc", tag="bank%d" % (PACK * h + r))
+                nc.tensor.matmul_mx(
+                    out=acc[:],
+                    lhsT=k_code[:, part].bitcast(FP8X4),
+                    lhsT_scale=k_scale[:, part],
+                    rhs=q_codes[h][:].bitcast(FP8X4),
+                    rhs_scale=q_scales[h][:],
+                    start=True,
+                    stop=True,
+                )
+                nc.scalar.activation(y[:, r, :], acc[:], GELU, bias=bias_cols[:, r : r + 1])
+            nc.sync.dma_start(y_rows[:, :, cols], y[:])
+
+            y_woven = held.tile([P, HALF, PACK], BF16, name="y_woven%d" % h, align_bytes=64)
+            nc.vector.tensor_copy(
+                y_woven[:].rearrange("p (c i) r -> p c r i", i=4),
+                y[:].rearrange("p r (c i) -> p c r i", i=4),
+            )
+            y_code = held.tile([P, HALF], I32, name="y_code%d" % h, align_bytes=64)
+            nc.vector.quantize_mx(
+                out=y_code[:].bitcast(FP8X4), scales=y_scale[:, cols], in_=y_woven[:].rearrange("p c r -> p (c r)")
+            )
+            nc.sync.dma_start(y_words[:, cols], y_code[:])
+
+        for quad in range(QUADS):
+            queue = nc.sync if quad % 2 else nc.scalar
+            queue.dma_start(
+                out_2[0, 4 * quad : 4 * quad + 4, :].bitcast(I32),
+                y_scale[32 * quad : 32 * quad + 4, :].bitcast(I32),
+            )

@@ -40,8 +40,12 @@ def tile_attend_plh_bgelu_topk_kernel(tc, qT, k_words, k_scales, nb, offs, out_0
         bias_pool = held.tile([P, POOL], F32, name="bias_pool")
         nc.vector.memset(bias_pool[0:BIAS_ROW, :], 0.0)
         nc.sync.dma_start(bias_pool[BIAS_ROW:P, :], nb[0:1, :])
+        q_rows = qT[0].rearrange("(p j) q -> p j q", j=PACK)
+        q_raws = [held.tile([P, PACK, HALF], F32, name="q_raw%d" % h) for h in range(NQ // HALF)]
+        nc.sync.dma_start(q_raws[0][:], q_rows[:, :, 0:HALF])
         for quad in range(QUADS):
-            nc.scalar.dma_start(
+            queue = nc.scalar if quad % 2 else nc.sync
+            queue.dma_start(
                 scale_pool[32 * quad : 32 * quad + 4, :].bitcast(I32),
                 k_scales[0, 4 * quad : 4 * quad + 4, :].bitcast(I32),
             )
@@ -50,8 +54,7 @@ def tile_attend_plh_bgelu_topk_kernel(tc, qT, k_words, k_scales, nb, offs, out_0
 
         word_pool = held.tile([P, POOL], I32, name="word_pool")
         nc.sync.dma_start(word_pool[:], k_words[0].rearrange("p n t -> p (n t)").bitcast(I32))
-        q_raw = held.tile([P, PACK, NQ], F32, name="q_raw")
-        nc.sync.dma_start(q_raw[:], qT[0].rearrange("(p j) q -> p j q", j=PACK))
+        nc.sync.dma_start(q_raws[1][:], q_rows[:, :, HALF:NQ])
 
         ident = held.tile([P, P], F32, name="ident")
         make_identity(nc, ident[:])
@@ -60,8 +63,11 @@ def tile_attend_plh_bgelu_topk_kernel(tc, qT, k_words, k_scales, nb, offs, out_0
         nc.vector.tensor_copy(bias_listed[:], bias_pool[:].indirect(offsets[:]))
         scale_listed = held.tile([P, SLOTS], U8, name="scale_listed", align_bytes=64)
         nc.vector.tensor_copy(scale_listed[:], scale_pool[:].indirect(offsets[:]))
-        word_listed = held.tile([P, SLOTS], I32, name="word_listed", align_bytes=64)
-        nc.vector.tensor_copy(word_listed[:].bitcast(U32), word_pool[:].bitcast(U32).indirect(offsets[:]))
+        k_code = held.tile([P, SLOTS], I32, name="k_code", align_bytes=64)
+        nc.vector.tensor_copy(
+            k_code[:].bitcast(U32).rearrange("p (r s) -> p s r", r=PACK),
+            word_pool[:].bitcast(U32).indirect(offsets[:]),
+        )
 
         bias_turned = psum.tile([P, PACK, P], F32, name="bias_turned", tag="bank7")
         for r in range(PACK):
@@ -74,11 +80,6 @@ def tile_attend_plh_bgelu_topk_kernel(tc, qT, k_words, k_scales, nb, offs, out_0
             k_scale[:].rearrange("p (r c i) -> p c r i", r=PACK, i=16),
             scale_listed[:].rearrange("p (c i r) -> p c r i", r=PACK, i=16),
         )
-        k_code = held.tile([P, SLOTS], I32, name="k_code", align_bytes=64)
-        nc.vector.tensor_copy(
-            k_code[:].rearrange("p (r c i) -> p c r i", r=PACK, i=4),
-            word_listed[:].rearrange("p (c i r) -> p c r i", r=PACK, i=4),
-        )
 
         y_scale = held.tile([P, NQ], U8, name="y_scale", align_bytes=64)
         y_rows = out_0.rearrange("(p r) q -> p r q", r=PACK)
@@ -87,11 +88,10 @@ def tile_attend_plh_bgelu_topk_kernel(tc, qT, k_words, k_scales, nb, offs, out_0
         q_codes = []
         q_scales = []
         for h in range(NQ // HALF):
-            cols = slice(h * HALF, (h + 1) * HALF)
             q_woven = held.tile([P, HALF, PACK], BF16, name="q_woven%d" % h, align_bytes=64)
             nc.scalar.copy(
                 q_woven[:].rearrange("p (c i) j -> p c j i", i=4),
-                q_raw[:, :, cols].rearrange("p j (c i) -> p c j i", i=4),
+                q_raws[h][:].rearrange("p j (c i) -> p c j i", i=4),
             )
             q_code = held.tile([P, HALF], U32, name="q_code%d" % h, align_bytes=64)
             q_scale = held.tile([P, HALF], U8, name="q_scale%d" % h, align_bytes=64)
@@ -117,7 +117,8 @@ def tile_attend_plh_bgelu_topk_kernel(tc, qT, k_words, k_scales, nb, offs, out_0
                     stop=True,
                 )
                 nc.scalar.activation(y[:, r, :], acc[:], GELU, bias=bias_cols[:, r : r + 1])
-            nc.sync.dma_start(y_rows[:, :, cols], y[:])
+            y_queue = nc.scalar if h else nc.sync
+            y_queue.dma_start(y_rows[:, :, cols], y[:])
 
             y_woven = held.tile([P, HALF, PACK], BF16, name="y_woven%d" % h, align_bytes=64)
             nc.vector.tensor_copy(

@@ -18,6 +18,7 @@ SLOTS = 512
 POOL = 2048
 NQ = 256
 HALF = 128
+PIECE = 64
 QUADS = 4
 BIAS_ROW = P - 1
 
@@ -33,16 +34,19 @@ def tile_attend_plh_bgelu_topk_kernel(tc, qT, k_words, k_scales, nb, offs, out_0
         offsets = held.tile([P, SLOTS // 16], U16, name="offsets")
         nc.sync.dma_start(offsets[:], offs)
 
-        scale_pool = held.tile([P, POOL], U8, name="scale_pool", align_bytes=64)
+        scale_pool = held.tile([P, POOL], U8, name="scale_pool", tag="scale0", align_bytes=64)
         nc.vector.memset(scale_pool[:].bitcast(I32), 0)
-        warm_in = held.tile([P, 1], F32, name="warm_in")
-        nc.vector.memset(warm_in[:], 0.0)
+        zeros = held.tile([P, P + 8], F32, name="zeros")
+        nc.vector.memset(zeros[:], 0.0)
+        ident = zeros[:, 0:P]
+        warm_in = zeros[:, P : P + 1]
+        make_identity(nc, ident, nomemset=True)
         bias_pool = held.tile([P, POOL], F32, name="bias_pool")
-        nc.vector.memset(bias_pool[0:BIAS_ROW, :], 0.0)
+        nc.vector.memset(bias_pool[0:BIAS_ROW, :].bitcast(I32), 0)
         nc.sync.dma_start(bias_pool[BIAS_ROW:P, :], nb[0:1, :])
         q_rows = qT[0].rearrange("(p j) q -> p j q", j=PACK)
         q_raws = [held.tile([P, PACK, HALF], F32, name="q_raw%d" % h) for h in range(NQ // HALF)]
-        nc.sync.dma_start(q_raws[0][:], q_rows[:, :, 0:HALF])
+        nc.scalar.dma_start(q_raws[0][:], q_rows[:, :, 0:HALF])
         for quad in range(QUADS):
             queue = nc.scalar if quad % 2 else nc.sync
             queue.dma_start(
@@ -50,14 +54,11 @@ def tile_attend_plh_bgelu_topk_kernel(tc, qT, k_words, k_scales, nb, offs, out_0
                 k_scales[0, 4 * quad : 4 * quad + 4, :].bitcast(I32),
             )
         warm_out = held.tile([P, 1], F32, name="warm_out")
-        nc.scalar.activation(warm_out[:], warm_in[:], GELU)
+        nc.scalar.activation(warm_out[:], warm_in, GELU)
 
         word_pool = held.tile([P, POOL], I32, name="word_pool")
         nc.sync.dma_start(word_pool[:], k_words[0].rearrange("p n t -> p (n t)").bitcast(I32))
         nc.sync.dma_start(q_raws[1][:], q_rows[:, :, HALF:NQ])
-
-        ident = held.tile([P, P], F32, name="ident")
-        make_identity(nc, ident[:])
 
         bias_listed = held.tile([P, SLOTS], F32, name="bias_listed")
         nc.vector.tensor_copy(bias_listed[:], bias_pool[:].indirect(offsets[:]))
@@ -71,35 +72,46 @@ def tile_attend_plh_bgelu_topk_kernel(tc, qT, k_words, k_scales, nb, offs, out_0
 
         bias_turned = psum.tile([P, PACK, P], F32, name="bias_turned", tag="bank7")
         for r in range(PACK):
-            nc.tensor.transpose(bias_turned[:, r, :], bias_listed[:, r:SLOTS:PACK], ident[:])
+            nc.tensor.transpose(bias_turned[:, r, :], bias_listed[:, r:SLOTS:PACK], ident)
         bias_cols = held.tile([P, PACK], F32, name="bias_cols")
         nc.scalar.copy(bias_cols[:], bias_turned[:, :, BIAS_ROW])
+
+
+        y_scale = held.tile([P, NQ], U8, name="y_scale", align_bytes=64)
+        y_rows = out_0.rearrange("(p r) q -> p r q", r=PACK)
+        y_words = out_1[0].rearrange("p q u -> p (q u)").bitcast(I32)
+
+        def weave_and_quantise(rows, woven, codes, scales):
+            pieces = [slice(c, c + PIECE) for c in range(0, HALF, PIECE)]
+            for piece in pieces:
+                nc.vector.tensor_copy(
+                    woven[:, piece, :].rearrange("p (c i) r -> p c r i", i=4),
+                    rows[:, :, piece].rearrange("p r (c i) -> p c r i", i=4),
+                )
+            for piece in pieces:
+                nc.vector.quantize_mx(
+                    out=codes[:, piece].bitcast(FP8X4),
+                    scales=scales[:, piece],
+                    in_=woven[:, piece, :].rearrange("p c r -> p (c r)"),
+                )
+
+        q_wovens = [held.tile([P, HALF, PACK], BF16, name="q_woven%d" % h, align_bytes=64) for h in range(2)]
+        q_codes = [held.tile([P, HALF], U32, name="q_code%d" % h, align_bytes=64) for h in range(2)]
+        q_scales = [held.tile([P, HALF], U8, name="q_scale%d" % h, tag="scale%d" % h, align_bytes=64) for h in range(2)]
+        nc.scalar.copy(
+            q_wovens[0][:].rearrange("p (c i) j -> p c j i", i=4),
+            q_raws[0][:].rearrange("p j (c i) -> p c j i", i=4),
+        )
+        nc.vector.quantize_mx(
+            out=q_codes[0][:].bitcast(FP8X4), scales=q_scales[0][:], in_=q_wovens[0][:].rearrange("p c j -> p (c j)")
+        )
 
         k_scale = held.tile([P, SLOTS], U8, name="k_scale", align_bytes=64)
         nc.vector.tensor_copy(
             k_scale[:].rearrange("p (r c i) -> p c r i", r=PACK, i=16),
             scale_listed[:].rearrange("p (c i r) -> p c r i", r=PACK, i=16),
         )
-
-        y_scale = held.tile([P, NQ], U8, name="y_scale", align_bytes=64)
-        y_rows = out_0.rearrange("(p r) q -> p r q", r=PACK)
-        y_words = out_1[0].rearrange("p q u -> p (q u)").bitcast(I32)
-
-        q_codes = []
-        q_scales = []
-        for h in range(NQ // HALF):
-            q_woven = held.tile([P, HALF, PACK], BF16, name="q_woven%d" % h, align_bytes=64)
-            nc.scalar.copy(
-                q_woven[:].rearrange("p (c i) j -> p c j i", i=4),
-                q_raws[h][:].rearrange("p j (c i) -> p c j i", i=4),
-            )
-            q_code = held.tile([P, HALF], U32, name="q_code%d" % h, align_bytes=64)
-            q_scale = held.tile([P, HALF], U8, name="q_scale%d" % h, align_bytes=64)
-            nc.vector.quantize_mx(
-                out=q_code[:].bitcast(FP8X4), scales=q_scale[:], in_=q_woven[:].rearrange("p c j -> p (c j)")
-            )
-            q_codes.append(q_code)
-            q_scales.append(q_scale)
+        weave_and_quantise(q_raws[1][:], q_wovens[1][:], q_codes[1][:], q_scales[1][:])
 
         for h in range(NQ // HALF):
             cols = slice(h * HALF, (h + 1) * HALF)
@@ -121,14 +133,8 @@ def tile_attend_plh_bgelu_topk_kernel(tc, qT, k_words, k_scales, nb, offs, out_0
             y_queue.dma_start(y_rows[:, :, cols], y[:])
 
             y_woven = held.tile([P, HALF, PACK], BF16, name="y_woven%d" % h, align_bytes=64)
-            nc.vector.tensor_copy(
-                y_woven[:].rearrange("p (c i) r -> p c r i", i=4),
-                y[:].rearrange("p r (c i) -> p c r i", i=4),
-            )
             y_code = held.tile([P, HALF], I32, name="y_code%d" % h, align_bytes=64)
-            nc.vector.quantize_mx(
-                out=y_code[:].bitcast(FP8X4), scales=y_scale[:, cols], in_=y_woven[:].rearrange("p c r -> p (c r)")
-            )
+            weave_and_quantise(y[:], y_woven[:], y_code[:], y_scale[:, cols])
             nc.sync.dma_start(y_words[:, cols], y_code[:])
 
         for quad in range(QUADS):

@@ -21,6 +21,7 @@ HALF = 128
 PIECE = 64
 QUADS = 4
 BIAS_ROW = P - 1
+EARLY = 512
 
 FLOPS = 2 * SLOTS * 512 * NQ
 
@@ -46,18 +47,20 @@ def tile_attend_plh_bgelu_topk_kernel(tc, qT, k_words, k_scales, nb, offs, out_0
         nc.sync.dma_start(bias_pool[BIAS_ROW:P, :], nb[0:1, :])
         q_rows = qT[0].rearrange("(p j) q -> p j q", j=PACK)
         q_raws = [held.tile([P, PACK, HALF], F32, name="q_raw%d" % h) for h in range(NQ // HALF)]
-        nc.scalar.dma_start(q_raws[0][:], q_rows[:, :, 0:HALF])
-        for quad in range(QUADS):
-            queue = nc.scalar if quad % 2 else nc.sync
+        word_pool = held.tile([P, POOL], I32, name="word_pool", tag="words", align_bytes=64)
+        word_rows = k_words[0].rearrange("p n t -> p (n t)").bitcast(I32)
+        nc.scalar.dma_start(word_pool[:, 0:EARLY], word_rows[:, 0:EARLY])
+        for row in range(QUADS):
+            queue = nc.scalar if row % 2 else nc.sync
             queue.dma_start(
-                scale_pool[32 * quad : 32 * quad + 4, :].bitcast(I32),
-                k_scales[0, 4 * quad : 4 * quad + 4, :].bitcast(I32),
+                scale_pool[row:P:32, :].bitcast(I32),
+                k_scales[0, row:16:4, :].bitcast(I32),
             )
         warm_out = held.tile([P, 1], F32, name="warm_out")
         nc.scalar.activation(warm_out[:], warm_in, GELU)
 
-        word_pool = held.tile([P, POOL], I32, name="word_pool")
-        nc.sync.dma_start(word_pool[:], k_words[0].rearrange("p n t -> p (n t)").bitcast(I32))
+        nc.sync.dma_start(word_pool[:, EARLY:POOL], word_rows[:, EARLY:POOL])
+        nc.sync.dma_start(q_raws[0][:], q_rows[:, :, 0:HALF])
         nc.sync.dma_start(q_raws[1][:], q_rows[:, :, HALF:NQ])
 
         bias_listed = held.tile([P, SLOTS], F32, name="bias_listed")
@@ -95,23 +98,28 @@ def tile_attend_plh_bgelu_topk_kernel(tc, qT, k_words, k_scales, nb, offs, out_0
                     in_=woven[:, piece, :].rearrange("p c r -> p (c r)"),
                 )
 
-        q_wovens = [held.tile([P, HALF, PACK], BF16, name="q_woven%d" % h, align_bytes=64) for h in range(2)]
+        q_wovens = [held.tile([P, HALF, PACK], BF16, name="q_woven%d" % h, tag="woven%d" % h, align_bytes=64) for h in range(2)]
         q_codes = [held.tile([P, HALF], U32, name="q_code%d" % h, align_bytes=64) for h in range(2)]
-        q_scales = [held.tile([P, HALF], U8, name="q_scale%d" % h, tag="scale%d" % h, align_bytes=64) for h in range(2)]
-        nc.scalar.copy(
-            q_wovens[0][:].rearrange("p (c i) j -> p c j i", i=4),
-            q_raws[0][:].rearrange("p j (c i) -> p c j i", i=4),
-        )
-        nc.vector.quantize_mx(
-            out=q_codes[0][:].bitcast(FP8X4), scales=q_scales[0][:], in_=q_wovens[0][:].rearrange("p c j -> p (c j)")
-        )
+        q_scales = [held.tile([P, HALF], U8, name="q_scale%d" % h, align_bytes=64) for h in range(2)]
+        for h in range(NQ // HALF):
+            nc.scalar.copy(
+                q_wovens[h][:].rearrange("p (c i) j -> p c j i", i=4),
+                q_raws[h][:].rearrange("p j (c i) -> p c j i", i=4),
+            )
 
-        k_scale = held.tile([P, SLOTS], U8, name="k_scale", align_bytes=64)
-        nc.vector.tensor_copy(
-            k_scale[:].rearrange("p (r c i) -> p c r i", r=PACK, i=16),
-            scale_listed[:].rearrange("p (c i r) -> p c r i", r=PACK, i=16),
-        )
-        weave_and_quantise(q_raws[1][:], q_wovens[1][:], q_codes[1][:], q_scales[1][:])
+        def quantise_queries(h):
+            nc.vector.quantize_mx(
+                out=q_codes[h][:].bitcast(FP8X4), scales=q_scales[h][:], in_=q_wovens[h][:].rearrange("p c j -> p (c j)")
+            )
+
+        quantise_queries(0)
+
+        k_scale_first = held.tile([P, P], U8, name="k_scale_first", align_bytes=64)
+        k_scale_rest = held.tile([P, SLOTS - P], U8, name="k_scale_rest", tag="woven0", align_bytes=64)
+        k_scale = [k_scale_first[:]] + [k_scale_rest[:, r * P : (r + 1) * P] for r in range(PACK - 1)]
+        for r in range(PACK):
+            nc.vector.tensor_copy(k_scale[r], scale_listed[:, r:SLOTS:PACK])
+        quantise_queries(1)
 
         for h in range(NQ // HALF):
             cols = slice(h * HALF, (h + 1) * HALF)
@@ -122,7 +130,7 @@ def tile_attend_plh_bgelu_topk_kernel(tc, qT, k_words, k_scales, nb, offs, out_0
                 nc.tensor.matmul_mx(
                     out=acc[:],
                     lhsT=k_code[:, part].bitcast(FP8X4),
-                    lhsT_scale=k_scale[:, part],
+                    lhsT_scale=k_scale[r],
                     rhs=q_codes[h][:].bitcast(FP8X4),
                     rhs_scale=q_scales[h][:],
                     start=True,

@@ -21,7 +21,7 @@ HALF = 128
 PIECE = 64
 QUADS = 4
 BIAS_ROW = P - 1
-EARLY = 512
+EARLY = 768
 
 FLOPS = 2 * SLOTS * 512 * NQ
 
@@ -44,15 +44,14 @@ def tile_attend_plh_bgelu_topk_kernel(tc, qT, k_words, k_scales, nb, offs, out_0
         make_identity(nc, ident, nomemset=True)
         bias_pool = held.tile([P, POOL], F32, name="bias_pool")
         nc.vector.memset(bias_pool[0:BIAS_ROW, :].bitcast(I32), 0)
-        nc.sync.dma_start(bias_pool[BIAS_ROW:P, :], nb[0:1, :])
+        nc.scalar.dma_start(bias_pool[BIAS_ROW:P, :], nb[0:1, :])
         q_rows = qT[0].rearrange("(p j) q -> p j q", j=PACK)
-        q_raws = [held.tile([P, PACK, HALF], F32, name="q_raw%d" % h) for h in range(NQ // HALF)]
+        q_raws = [held.tile([P, PACK, HALF], F32, name="q_raw%d" % h, tag="raw%d" % h, align_bytes=64) for h in range(NQ // HALF)]
         word_pool = held.tile([P, POOL], I32, name="word_pool", tag="words", align_bytes=64)
         word_rows = k_words[0].rearrange("p n t -> p (n t)").bitcast(I32)
-        nc.scalar.dma_start(word_pool[:, 0:EARLY], word_rows[:, 0:EARLY])
+        nc.sync.dma_start(word_pool[:, 0:EARLY], word_rows[:, 0:EARLY])
         for row in range(QUADS):
-            queue = nc.scalar if row % 2 else nc.sync
-            queue.dma_start(
+            nc.sync.dma_start(
                 scale_pool[row:P:32, :].bitcast(I32),
                 k_scales[0, row:16:4, :].bitcast(I32),
             )
@@ -98,7 +97,7 @@ def tile_attend_plh_bgelu_topk_kernel(tc, qT, k_words, k_scales, nb, offs, out_0
                     in_=woven[:, piece, :].rearrange("p c r -> p (c r)"),
                 )
 
-        q_wovens = [held.tile([P, HALF, PACK], BF16, name="q_woven%d" % h, tag="woven%d" % h, align_bytes=64) for h in range(2)]
+        q_wovens = [held.tile([P, HALF, PACK], BF16, name="q_woven%d" % h, align_bytes=64) for h in range(2)]
         q_codes = [held.tile([P, HALF], U32, name="q_code%d" % h, align_bytes=64) for h in range(2)]
         q_scales = [held.tile([P, HALF], U8, name="q_scale%d" % h, align_bytes=64) for h in range(2)]
         for h in range(NQ // HALF):
@@ -114,9 +113,8 @@ def tile_attend_plh_bgelu_topk_kernel(tc, qT, k_words, k_scales, nb, offs, out_0
 
         quantise_queries(0)
 
-        k_scale_first = held.tile([P, P], U8, name="k_scale_first", align_bytes=64)
-        k_scale_rest = held.tile([P, SLOTS - P], U8, name="k_scale_rest", tag="woven0", align_bytes=64)
-        k_scale = [k_scale_first[:]] + [k_scale_rest[:, r * P : (r + 1) * P] for r in range(PACK - 1)]
+        k_scale_dealt = held.tile([P, SLOTS], U8, name="k_scale_dealt", tag="raw0", align_bytes=64)
+        k_scale = [k_scale_dealt[:, r * P : (r + 1) * P] for r in range(PACK)]
         for r in range(PACK):
             nc.vector.tensor_copy(k_scale[r], scale_listed[:, r:SLOTS:PACK])
         quantise_queries(1)

@@ -21,7 +21,8 @@ HALF = 128
 PIECE = 64
 QUADS = 4
 BIAS_ROW = P - 1
-EARLY = 768
+SCALE_ROW = P - 16
+EARLY = 512
 
 FLOPS = 2 * SLOTS * 512 * NQ
 
@@ -30,42 +31,47 @@ def tile_attend_plh_bgelu_topk_kernel(tc, qT, k_words, k_scales, nb, offs, out_0
     nc = tc.nc
     with ExitStack() as ctx:
         held = ctx.enter_context(tc.tile_pool(name="held", bufs=1))
+        reused = ctx.enter_context(tc.tile_pool(name="reused", bufs=1))
         psum = ctx.enter_context(tc.psum_pool(name="psum", bufs=1))
 
         offsets = held.tile([P, SLOTS // 16], U16, name="offsets")
         nc.sync.dma_start(offsets[:], offs)
 
-        scale_pool = held.tile([P, POOL], U8, name="scale_pool", tag="scale0", align_bytes=64)
-        nc.vector.memset(scale_pool[:].bitcast(I32), 0)
-        zeros = held.tile([P, P + 8], F32, name="zeros")
-        nc.vector.memset(zeros[:], 0.0)
-        ident = zeros[:, 0:P]
-        warm_in = zeros[:, P : P + 1]
-        make_identity(nc, ident, nomemset=True)
+        scale_pool = held.tile([P, POOL], U8, name="scale_pool", align_bytes=64)
+        nc.vector.memset(scale_pool[0:SCALE_ROW, :].bitcast(I32), 0)
+        nc.sync.dma_start(scale_pool[SCALE_ROW:P, :].bitcast(I32), k_scales[0].bitcast(I32))
+        ident = held.tile([P, P], F32, name="ident")
+        nc.vector.memset(ident[:], 0.0)
+        make_identity(nc, ident[:], nomemset=True)
         bias_pool = held.tile([P, POOL], F32, name="bias_pool")
         nc.vector.memset(bias_pool[0:BIAS_ROW, :].bitcast(I32), 0)
-        nc.scalar.dma_start(bias_pool[BIAS_ROW:P, :], nb[0:1, :])
         q_rows = qT[0].rearrange("(p j) q -> p j q", j=PACK)
-        q_raws = [held.tile([P, PACK, HALF], F32, name="q_raw%d" % h, tag="raw%d" % h, align_bytes=64) for h in range(NQ // HALF)]
-        word_pool = held.tile([P, POOL], I32, name="word_pool", tag="words", align_bytes=64)
+        q_raw_first = reused.tile([P, PACK, HALF], F32, name="q_raw_first", offset=0, align_bytes=64)
+        word_pool = held.tile([P, POOL], I32, name="word_pool")
         word_rows = k_words[0].rearrange("p n t -> p (n t)").bitcast(I32)
-        nc.sync.dma_start(word_pool[:, 0:EARLY], word_rows[:, 0:EARLY])
-        for row in range(QUADS):
-            nc.sync.dma_start(
-                scale_pool[row:P:32, :].bitcast(I32),
-                k_scales[0, row:16:4, :].bitcast(I32),
-            )
+        scale_placed = held.tile([P, SLOTS], U8, name="scale_placed", tag="placed", align_bytes=64)
+        nc.vector.memset(scale_placed[:].bitcast(I32), 0)
         warm_out = held.tile([P, 1], F32, name="warm_out")
-        nc.scalar.activation(warm_out[:], warm_in, GELU)
+        nc.scalar.activation(warm_out[:], ident[:, 0:1], GELU)
 
+        nc.sync.dma_start(word_pool[:, 0:EARLY], word_rows[:, 0:EARLY])
+        nc.sync.dma_start(bias_pool[BIAS_ROW:P, :], nb[0:1, :])
         nc.sync.dma_start(word_pool[:, EARLY:POOL], word_rows[:, EARLY:POOL])
-        nc.sync.dma_start(q_raws[0][:], q_rows[:, :, 0:HALF])
-        nc.sync.dma_start(q_raws[1][:], q_rows[:, :, HALF:NQ])
+        nc.sync.dma_start(q_raw_first[:], q_rows[:, :, 0:HALF])
+        q_raw_second = held.tile([P, PACK, HALF], F32, name="q_raw_second")
+        nc.sync.dma_start(q_raw_second[:], q_rows[:, :, HALF:NQ])
 
-        bias_listed = held.tile([P, SLOTS], F32, name="bias_listed")
-        nc.vector.tensor_copy(bias_listed[:], bias_pool[:].indirect(offsets[:]))
         scale_listed = held.tile([P, SLOTS], U8, name="scale_listed", align_bytes=64)
         nc.vector.tensor_copy(scale_listed[:], scale_pool[:].indirect(offsets[:]))
+        for quad in range(QUADS):
+            first = SCALE_ROW + 4 * quad
+            nc.sync.dma_start(
+                scale_placed[32 * quad : 32 * quad + 4, :].bitcast(I32),
+                scale_listed[first : first + 4, :].bitcast(I32),
+            )
+        q_raws = [q_raw_first, q_raw_second]
+        bias_listed = held.tile([P, SLOTS], F32, name="bias_listed")
+        nc.vector.tensor_copy(bias_listed[:], bias_pool[:].indirect(offsets[:]))
         k_code = held.tile([P, SLOTS], I32, name="k_code", align_bytes=64)
         nc.vector.tensor_copy(
             k_code[:].bitcast(U32).rearrange("p (r s) -> p s r", r=PACK),
@@ -74,12 +80,11 @@ def tile_attend_plh_bgelu_topk_kernel(tc, qT, k_words, k_scales, nb, offs, out_0
 
         bias_turned = psum.tile([P, PACK, P], F32, name="bias_turned", tag="bank7")
         for r in range(PACK):
-            nc.tensor.transpose(bias_turned[:, r, :], bias_listed[:, r:SLOTS:PACK], ident)
-        bias_cols = held.tile([P, PACK], F32, name="bias_cols")
-        nc.scalar.copy(bias_cols[:], bias_turned[:, :, BIAS_ROW])
+            nc.tensor.transpose(bias_turned[:, r, :], bias_listed[:, r:SLOTS:PACK], ident[:])
 
 
         y_scale = held.tile([P, NQ], U8, name="y_scale", align_bytes=64)
+        y_code = held.tile([P, NQ], I32, name="y_code", align_bytes=64)
         y_rows = out_0.rearrange("(p r) q -> p r q", r=PACK)
         y_words = out_1[0].rearrange("p q u -> p (q u)").bitcast(I32)
 
@@ -99,12 +104,18 @@ def tile_attend_plh_bgelu_topk_kernel(tc, qT, k_words, k_scales, nb, offs, out_0
 
         q_wovens = [held.tile([P, HALF, PACK], BF16, name="q_woven%d" % h, align_bytes=64) for h in range(2)]
         q_codes = [held.tile([P, HALF], U32, name="q_code%d" % h, align_bytes=64) for h in range(2)]
-        q_scales = [held.tile([P, HALF], U8, name="q_scale%d" % h, align_bytes=64) for h in range(2)]
+        q_scales = [
+            held.tile([P, HALF], U8, name="q_scale_first", align_bytes=64),
+            held.tile([P, HALF], U8, name="q_scale_second", tag="placed", align_bytes=64),
+        ]
         for h in range(NQ // HALF):
             nc.scalar.copy(
                 q_wovens[h][:].rearrange("p (c i) j -> p c j i", i=4),
                 q_raws[h][:].rearrange("p j (c i) -> p c j i", i=4),
             )
+
+        bias_cols = reused.tile([P, PACK], F32, name="bias_cols", offset=SLOTS, align_bytes=64)
+        nc.scalar.copy(bias_cols[:], bias_turned[:, :, BIAS_ROW])
 
         def quantise_queries(h):
             nc.vector.quantize_mx(
@@ -113,10 +124,10 @@ def tile_attend_plh_bgelu_topk_kernel(tc, qT, k_words, k_scales, nb, offs, out_0
 
         quantise_queries(0)
 
-        k_scale_dealt = held.tile([P, SLOTS], U8, name="k_scale_dealt", tag="raw0", align_bytes=64)
+        k_scale_dealt = reused.tile([P, SLOTS], U8, name="k_scale_dealt", offset=0, align_bytes=64)
         k_scale = [k_scale_dealt[:, r * P : (r + 1) * P] for r in range(PACK)]
         for r in range(PACK):
-            nc.vector.tensor_copy(k_scale[r], scale_listed[:, r:SLOTS:PACK])
+            nc.vector.tensor_copy(k_scale[r], scale_placed[:, r:SLOTS:PACK])
         quantise_queries(1)
 
         for h in range(NQ // HALF):
@@ -135,14 +146,13 @@ def tile_attend_plh_bgelu_topk_kernel(tc, qT, k_words, k_scales, nb, offs, out_0
                     stop=True,
                 )
                 nc.scalar.activation(y[:, r, :], acc[:], GELU, bias=bias_cols[:, r : r + 1])
-            y_queue = nc.scalar if h else nc.sync
-            y_queue.dma_start(y_rows[:, :, cols], y[:])
+                if r % 2:
+                    nc.sync.dma_start(y_rows[:, r - 1 : r + 1, cols], y[:, r - 1 : r + 1, :])
 
             y_woven = held.tile([P, HALF, PACK], BF16, name="y_woven%d" % h, align_bytes=64)
-            y_code = held.tile([P, HALF], I32, name="y_code%d" % h, align_bytes=64)
-            weave_and_quantise(y[:], y_woven[:], y_code[:], y_scale[:, cols])
-            nc.sync.dma_start(y_words[:, cols], y_code[:])
+            weave_and_quantise(y[:], y_woven[:], y_code[:, cols], y_scale[:, cols])
 
+        nc.sync.dma_start(y_words, y_code[:])
         for quad in range(QUADS):
             queue = nc.sync if quad % 2 else nc.scalar
             queue.dma_start(

@@ -37,9 +37,11 @@ def tile_attend_plh_bgelu_topk_kernel(tc, qT, k_words, k_scales, nb, offs, out_0
         offsets = held.tile([P, SLOTS // 16], U16, name="offsets")
         nc.sync.dma_start(offsets[:], offs)
 
+        warm_in = held.tile([P, 1], F32, name="warm_in")
+        nc.vector.memset(warm_in[:], 0.0)
         scale_pool = held.tile([P, POOL], U8, name="scale_pool", align_bytes=64)
         nc.vector.memset(scale_pool[0:SCALE_ROW, :].bitcast(I32), 0)
-        nc.sync.dma_start(scale_pool[SCALE_ROW:P, :].bitcast(I32), k_scales[0].bitcast(I32))
+        nc.sync.dma_start(scale_pool[SCALE_ROW : SCALE_ROW + 16, :].bitcast(I32), k_scales[0].bitcast(I32))
         ident = held.tile([P, P], F32, name="ident")
         nc.vector.memset(ident[:], 0.0)
         make_identity(nc, ident[:], nomemset=True)
@@ -52,7 +54,7 @@ def tile_attend_plh_bgelu_topk_kernel(tc, qT, k_words, k_scales, nb, offs, out_0
         scale_placed = held.tile([P, SLOTS], U8, name="scale_placed", tag="placed", align_bytes=64)
         nc.vector.memset(scale_placed[:].bitcast(I32), 0)
         warm_out = held.tile([P, 1], F32, name="warm_out")
-        nc.scalar.activation(warm_out[:], ident[:, 0:1], GELU)
+        nc.scalar.activation(warm_out[:], warm_in[:], GELU)
 
         nc.sync.dma_start(word_pool[:, 0:EARLY], word_rows[:, 0:EARLY])
         nc.sync.dma_start(bias_pool[BIAS_ROW:P, :], nb[0:1, :])
@@ -65,7 +67,7 @@ def tile_attend_plh_bgelu_topk_kernel(tc, qT, k_words, k_scales, nb, offs, out_0
         nc.vector.tensor_copy(scale_listed[:], scale_pool[:].indirect(offsets[:]))
         for quad in range(QUADS):
             first = SCALE_ROW + 4 * quad
-            nc.sync.dma_start(
+            nc.scalar.dma_start(
                 scale_placed[32 * quad : 32 * quad + 4, :].bitcast(I32),
                 scale_listed[first : first + 4, :].bitcast(I32),
             )

@@ -90,19 +90,18 @@ def tile_attend_plh_bgelu_topk_kernel(tc, qT, k_words, k_scales, nb, offs, out_0
         y_rows = out_0.rearrange("(p r) q -> p r q", r=PACK)
         y_words = out_1[0].rearrange("p q u -> p (q u)").bitcast(I32)
 
-        def weave_and_quantise(rows, woven, codes, scales):
-            pieces = [slice(c, c + PIECE) for c in range(0, HALF, PIECE)]
-            for piece in pieces:
-                nc.vector.tensor_copy(
-                    woven[:, piece, :].rearrange("p (c i) r -> p c r i", i=4),
-                    rows[:, :, piece].rearrange("p r (c i) -> p c r i", i=4),
-                )
-            for piece in pieces:
-                nc.vector.quantize_mx(
-                    out=codes[:, piece].bitcast(FP8X4),
-                    scales=scales[:, piece],
-                    in_=woven[:, piece, :].rearrange("p c r -> p (c r)"),
-                )
+        def weave(rows, woven):
+            nc.vector.tensor_copy(
+                woven.rearrange("p (c i) r -> p c r i", i=4),
+                rows.rearrange("p r (c i) -> p c r i", i=4),
+            )
+
+        def quantise_result(woven, cols):
+            nc.vector.quantize_mx(
+                out=y_code[:, cols].bitcast(FP8X4),
+                scales=y_scale[:, cols],
+                in_=woven.rearrange("p c r -> p (c r)"),
+            )
 
         q_wovens = [held.tile([P, HALF, PACK], BF16, name="q_woven%d" % h, align_bytes=64) for h in range(2)]
         q_codes = [held.tile([P, HALF], U32, name="q_code%d" % h, align_bytes=64) for h in range(2)]
@@ -132,12 +131,16 @@ def tile_attend_plh_bgelu_topk_kernel(tc, qT, k_words, k_scales, nb, offs, out_0
             nc.vector.tensor_copy(k_scale[r], scale_placed[:, r:SLOTS:PACK])
         quantise_queries(1)
 
-        for h in range(NQ // HALF):
+        y_pairs = [held.tile([P, 2, NQ], F32, name="y_pair%d" % u) for u in range(2)]
+        y_wovens = [held.tile([P, HALF, PACK], BF16, name="y_woven%d" % h, align_bytes=64) for h in range(2)]
+        steps = [(0, 0), (0, 1), (1, 1), (1, 0)]
+        for step, (h, u) in enumerate(steps):
             cols = slice(h * HALF, (h + 1) * HALF)
-            y = held.tile([P, PACK, HALF], F32, name="y%d" % h)
-            for r in range(PACK):
+            y = y_pairs[u]
+            for e in range(2):
+                r = 2 * u + e
                 part = slice(r * P, (r + 1) * P)
-                acc = psum.tile([P, HALF], F32, name="acc", tag="bank%d" % (PACK * h + r))
+                acc = psum.tile([P, HALF], F32, name="acc", tag="bank%d" % (2 * step + e))
                 nc.tensor.matmul_mx(
                     out=acc[:],
                     lhsT=k_code[:, part].bitcast(FP8X4),
@@ -147,12 +150,21 @@ def tile_attend_plh_bgelu_topk_kernel(tc, qT, k_words, k_scales, nb, offs, out_0
                     start=True,
                     stop=True,
                 )
-                nc.scalar.activation(y[:, r, :], acc[:], GELU, bias=bias_cols[:, r : r + 1])
-                if r % 2:
-                    nc.sync.dma_start(y_rows[:, r - 1 : r + 1, cols], y[:, r - 1 : r + 1, :])
-
-            y_woven = held.tile([P, HALF, PACK], BF16, name="y_woven%d" % h, align_bytes=64)
-            weave_and_quantise(y[:], y_woven[:], y_code[:, cols], y_scale[:, cols])
+                nc.scalar.activation(y[:, e, cols], acc[:], GELU, bias=bias_cols[:, r : r + 1])
+                if (h, u) == (1, 1):
+                    nc.sync.dma_start(y_rows[:, r, :], y[:, e, :])
+            if u == 0:
+                nc.sync.dma_start(y_rows[:, 0:2, cols], y[:, :, cols])
+            places = slice(2 * u, 2 * u + 2)
+            if step < len(steps) - 1:
+                weave(y[:, :, cols], y_wovens[h][:, :, places])
+                if step == 1:
+                    quantise_result(y_wovens[h][:], cols)
+            else:
+                for c in range(0, HALF, PIECE):
+                    weave(y[:, :, h * HALF + c : h * HALF + c + PIECE], y_wovens[h][:, c : c + PIECE, places])
+                for c in range(0, HALF, PIECE):
+                    quantise_result(y_wovens[h][:, c : c + PIECE, :], slice(h * HALF + c, h * HALF + c + PIECE))
 
         nc.sync.dma_start(y_words, y_code[:])
         for quad in range(QUADS):

@@ -37,24 +37,22 @@ def tile_attend_plh_bgelu_topk_kernel(tc, qT, k_words, k_scales, nb, offs, out_0
         offsets = held.tile([P, SLOTS // 16], U16, name="offsets")
         nc.sync.dma_start(offsets[:], offs)
 
-        warm_in = held.tile([P, 1], F32, name="warm_in")
-        nc.vector.memset(warm_in[:], 0.0)
+        ident = held.tile([P, P], F32, name="ident")
+        nc.vector.memset(ident[:], 0.0)
+        warm_out = held.tile([P, 1], F32, name="warm_out")
+        nc.scalar.activation(warm_out[:], ident[:, 0:1], GELU)
+        make_identity(nc, ident[:], nomemset=True)
         scale_pool = held.tile([P, POOL], U8, name="scale_pool", align_bytes=64)
         nc.vector.memset(scale_pool[0:SCALE_ROW, :].bitcast(I32), 0)
         nc.sync.dma_start(scale_pool[SCALE_ROW : SCALE_ROW + 16, :].bitcast(I32), k_scales[0].bitcast(I32))
-        ident = held.tile([P, P], F32, name="ident")
-        nc.vector.memset(ident[:], 0.0)
-        make_identity(nc, ident[:], nomemset=True)
+        scale_placed = held.tile([P, SLOTS], U8, name="scale_placed", tag="placed", align_bytes=64)
+        nc.vector.memset(scale_placed[:].bitcast(I32), 0)
         bias_pool = held.tile([P, POOL], F32, name="bias_pool")
         nc.vector.memset(bias_pool[0:BIAS_ROW, :].bitcast(I32), 0)
         q_rows = qT[0].rearrange("(p j) q -> p j q", j=PACK)
         q_raw_first = reused.tile([P, PACK, HALF], F32, name="q_raw_first", offset=0, align_bytes=64)
         word_pool = held.tile([P, POOL], I32, name="word_pool")
         word_rows = k_words[0].rearrange("p n t -> p (n t)").bitcast(I32)
-        scale_placed = held.tile([P, SLOTS], U8, name="scale_placed", tag="placed", align_bytes=64)
-        nc.vector.memset(scale_placed[:].bitcast(I32), 0)
-        warm_out = held.tile([P, 1], F32, name="warm_out")
-        nc.scalar.activation(warm_out[:], warm_in[:], GELU)
 
         nc.sync.dma_start(word_pool[:, 0:EARLY], word_rows[:, 0:EARLY])
         nc.sync.dma_start(bias_pool[BIAS_ROW:P, :], nb[0:1, :])

@@ -90,8 +90,8 @@ def tile_attend_plh_bgelu_topk_kernel(tc, qT, k_words, k_scales, nb, offs, out_0
 
         def weave(rows, woven):
             nc.vector.tensor_copy(
-                woven.rearrange("p (c i) r -> p c r i", i=4),
-                rows.rearrange("p r (c i) -> p c r i", i=4),
+                woven.rearrange("p (c i) r -> p c r i", i=2),
+                rows.rearrange("p r (c i) -> p c r i", i=2),
             )
 
         def quantise_result(woven, cols):

@@ -11,6 +11,7 @@ U16 = mybir.dt.uint16
 U8 = mybir.dt.uint8
 FP8X4 = mybir.dt.float8_e4m3fn_x4
 GELU = mybir.ActivationFunctionType.Gelu_apprx_tanh
+COPY = mybir.ActivationFunctionType.Copy
 
 P = 128
 PACK = 4
@@ -37,6 +38,8 @@ def tile_attend_plh_bgelu_topk_kernel(tc, qT, k_words, k_scales, nb, offs, out_0
         offsets = held.tile([P, SLOTS // 16], U16, name="offsets")
         nc.sync.dma_start(offsets[:], offs)
 
+        bias_pool = held.tile([P, POOL], F32, name="bias_pool")
+        nc.scalar.dma_start(bias_pool[BIAS_ROW:P, :], nb[0:1, :])
         ident = held.tile([P, P], F32, name="ident")
         nc.vector.memset(ident[:], 0.0)
         warm_out = held.tile([P, 1], F32, name="warm_out")
@@ -47,7 +50,6 @@ def tile_attend_plh_bgelu_topk_kernel(tc, qT, k_words, k_scales, nb, offs, out_0
         nc.sync.dma_start(scale_pool[SCALE_ROW : SCALE_ROW + 16, :].bitcast(I32), k_scales[0].bitcast(I32))
         scale_placed = held.tile([P, SLOTS], U8, name="scale_placed", tag="placed", align_bytes=64)
         nc.vector.memset(scale_placed[:].bitcast(I32), 0)
-        bias_pool = held.tile([P, POOL], F32, name="bias_pool")
         nc.vector.memset(bias_pool[0:BIAS_ROW, :].bitcast(I32), 0)
         q_rows = qT[0].rearrange("(p j) q -> p j q", j=PACK)
         q_raw_first = reused.tile([P, PACK, HALF], F32, name="q_raw_first", offset=0, align_bytes=64)
@@ -55,7 +57,6 @@ def tile_attend_plh_bgelu_topk_kernel(tc, qT, k_words, k_scales, nb, offs, out_0
         word_rows = k_words[0].rearrange("p n t -> p (n t)").bitcast(I32)
 
         nc.sync.dma_start(word_pool[:, 0:EARLY], word_rows[:, 0:EARLY])
-        nc.sync.dma_start(bias_pool[BIAS_ROW:P, :], nb[0:1, :])
         nc.sync.dma_start(word_pool[:, EARLY:POOL], word_rows[:, EARLY:POOL])
         nc.sync.dma_start(q_raw_first[:], q_rows[:, :, 0:HALF])
         q_raw_second = held.tile([P, PACK, HALF], F32, name="q_raw_second")
@@ -65,13 +66,13 @@ def tile_attend_plh_bgelu_topk_kernel(tc, qT, k_words, k_scales, nb, offs, out_0
         nc.vector.tensor_copy(scale_listed[:], scale_pool[:].indirect(offsets[:]))
         for quad in range(QUADS):
             first = SCALE_ROW + 4 * quad
-            nc.scalar.dma_start(
+            nc.sync.dma_start(
                 scale_placed[32 * quad : 32 * quad + 4, :].bitcast(I32),
                 scale_listed[first : first + 4, :].bitcast(I32),
             )
         q_raws = [q_raw_first, q_raw_second]
         bias_listed = held.tile([P, SLOTS], F32, name="bias_listed")
-        nc.vector.tensor_copy(bias_listed[:], bias_pool[:].indirect(offsets[:]))
+        nc.scalar.activation(bias_listed[:], bias_pool[:].indirect(offsets[:]), COPY)
         k_code = held.tile([P, SLOTS], I32, name="k_code", align_bytes=64)
         nc.vector.tensor_copy(
             k_code[:].bitcast(U32).rearrange("p (r s) -> p s r", r=PACK),

@@ -38,6 +38,8 @@ def tile_attend_plh_bgelu_topk_kernel(tc, qT, k_words, k_scales, nb, offs, out_0
         offsets = held.tile([P, SLOTS // 16], U16, name="offsets")
         nc.sync.dma_start(offsets[:], offs)
 
+        scale_pool = held.tile([P, POOL], U8, name="scale_pool", align_bytes=64)
+        nc.scalar.dma_start(scale_pool[SCALE_ROW : SCALE_ROW + 16, :].bitcast(I32), k_scales[0].bitcast(I32))
         bias_pool = held.tile([P, POOL], F32, name="bias_pool")
         nc.scalar.dma_start(bias_pool[BIAS_ROW:P, :], nb[0:1, :])
         ident = held.tile([P, P], F32, name="ident")
@@ -45,9 +47,7 @@ def tile_attend_plh_bgelu_topk_kernel(tc, qT, k_words, k_scales, nb, offs, out_0
         warm_out = held.tile([P, 1], F32, name="warm_out")
         nc.scalar.activation(warm_out[:], ident[:, 0:1], GELU)
         make_identity(nc, ident[:], nomemset=True)
-        scale_pool = held.tile([P, POOL], U8, name="scale_pool", align_bytes=64)
         nc.vector.memset(scale_pool[0:SCALE_ROW, :].bitcast(I32), 0)
-        nc.sync.dma_start(scale_pool[SCALE_ROW : SCALE_ROW + 16, :].bitcast(I32), k_scales[0].bitcast(I32))
         scale_placed = held.tile([P, SLOTS], U8, name="scale_placed", tag="placed", align_bytes=64)
         nc.vector.memset(scale_placed[:].bitcast(I32), 0)
         nc.vector.memset(bias_pool[0:BIAS_ROW, :].bitcast(I32), 0)

@@ -150,11 +150,8 @@ def tile_attend_plh_bgelu_topk_kernel(tc, qT, k_words, k_scales, nb, offs, out_0
                     stop=True,
                 )
                 nc.scalar.activation(y[:, e, cols], acc[:], GELU, bias=bias_cols[:, r : r + 1])
-                if (h, u) == (1, 1):
-                    nc.sync.dma_start(y_rows[:, r, :], y[:, e, :])
-            if u == 0:
-                nc.sync.dma_start(y_rows[:, 0:2, cols], y[:, :, cols])
             places = slice(2 * u, 2 * u + 2)
+            nc.sync.dma_start(y_rows[:, places, cols], y[:, :, cols])
             if step < len(steps) - 1:
                 weave(y[:, :, cols], y_wovens[h][:, :, places])
                 if step == 1:

@@ -130,12 +130,12 @@ def tile_attend_plh_bgelu_topk_kernel(tc, qT, k_words, k_scales, nb, offs, out_0
             nc.vector.tensor_copy(k_scale[r], scale_placed[:, r:SLOTS:PACK])
         quantise_queries(1)
 
-        y_pairs = [held.tile([P, 2, NQ], F32, name="y_pair%d" % u) for u in range(2)]
+        y_all = held.tile([P, PACK, NQ], F32, name="y_all")
         y_wovens = [held.tile([P, HALF, PACK], BF16, name="y_woven%d" % h, align_bytes=64) for h in range(2)]
         steps = [(0, 0), (0, 1), (1, 1), (1, 0)]
         for step, (h, u) in enumerate(steps):
             cols = slice(h * HALF, (h + 1) * HALF)
-            y = y_pairs[u]
+            y = y_all[:, 2 * u : 2 * u + 2, :]
             for e in range(2):
                 r = 2 * u + e
                 part = slice(r * P, (r + 1) * P)
@@ -150,8 +150,13 @@ def tile_attend_plh_bgelu_topk_kernel(tc, qT, k_words, k_scales, nb, offs, out_0
                     stop=True,
                 )
                 nc.scalar.activation(y[:, e, cols], acc[:], GELU, bias=bias_cols[:, r : r + 1])
+                if (h, r) == (0, 0):
+                    nc.sync.dma_start(y_rows[:, 0, cols], y_all[:, 0, cols])
             places = slice(2 * u, 2 * u + 2)
-            nc.sync.dma_start(y_rows[:, places, cols], y[:, :, cols])
+            if h == 1:
+                nc.sync.dma_start(y_rows[:, places, cols], y[:, :, cols])
+            elif u == 1:
+                nc.sync.dma_start(y_rows[:, 1:PACK, cols], y_all[:, 1:PACK, cols])
             if step < len(steps) - 1:
                 weave(y[:, :, cols], y_wovens[h][:, :, places])
                 if step == 1:

@@ -84,7 +84,6 @@ def tile_attend_plh_bgelu_topk_kernel(tc, qT, k_words, k_scales, nb, offs, out_0
             nc.tensor.transpose(bias_turned[:, r, :], bias_listed[:, r:SLOTS:PACK], ident[:])
 
 
-        y_scale = held.tile([P, NQ], U8, name="y_scale", align_bytes=64)
         y_code = held.tile([P, NQ], I32, name="y_code", align_bytes=64)
         y_rows = out_0.rearrange("(p r) q -> p r q", r=PACK)
         y_words = out_1[0].rearrange("p q u -> p (q u)").bitcast(I32)
@@ -131,6 +130,7 @@ def tile_attend_plh_bgelu_topk_kernel(tc, qT, k_words, k_scales, nb, offs, out_0
         quantise_queries(1)
 
         y_all = held.tile([P, PACK, NQ], F32, name="y_all")
+        y_scale = reused.tile([P, NQ], U8, name="y_scale", offset=SLOTS, align_bytes=64)
         y_wovens = [held.tile([P, HALF, PACK], BF16, name="y_woven%d" % h, align_bytes=64) for h in range(2)]
         steps = [(0, 0), (0, 1), (1, 1), (1, 0)]
         for step, (h, u) in enumerate(steps):
@@ -149,7 +149,12 @@ def tile_attend_plh_bgelu_topk_kernel(tc, qT, k_words, k_scales, nb, offs, out_0
                     start=True,
                     stop=True,
                 )
-                nc.scalar.activation(y[:, e, cols], acc[:], GELU, bias=bias_cols[:, r : r + 1])
+                last = step == len(steps) - 1 and e == 1
+                width = PIECE if last else HALF
+                for c in range(0, HALF, width):
+                    nc.scalar.activation(
+                        y[:, e, h * HALF + c : h * HALF + c + width], acc[:, c : c + width], GELU, bias=bias_cols[:, r : r + 1]
+                    )
                 if (h, r) == (0, 0):
                     nc.sync.dma_start(y_rows[:, 0, cols], y_all[:, 0, cols])
             places = slice(2 * u, 2 * u + 2)
@@ -159,11 +164,10 @@ def tile_attend_plh_bgelu_topk_kernel(tc, qT, k_words, k_scales, nb, offs, out_0
                 nc.sync.dma_start(y_rows[:, 1:PACK, cols], y_all[:, 1:PACK, cols])
             if step < len(steps) - 1:
                 weave(y[:, :, cols], y_wovens[h][:, :, places])
-                if step == 1:
-                    quantise_result(y_wovens[h][:], cols)
             else:
                 for c in range(0, HALF, PIECE):
                     weave(y[:, :, h * HALF + c : h * HALF + c + PIECE], y_wovens[h][:, c : c + PIECE, places])
+                quantise_result(y_wovens[0][:], slice(0, HALF))
                 for c in range(0, HALF, PIECE):
                     quantise_result(y_wovens[h][:, c : c + PIECE, :], slice(h * HALF + c, h * HALF + c + PIECE))
 

@@ -132,12 +132,17 @@ def tile_attend_plh_bgelu_topk_kernel(tc, qT, k_words, k_scales, nb, offs, out_0
         y_all = held.tile([P, PACK, NQ], F32, name="y_all")
         y_scale = reused.tile([P, NQ], U8, name="y_scale", offset=SLOTS, align_bytes=64)
         y_wovens = [held.tile([P, HALF, PACK], BF16, name="y_woven%d" % h, align_bytes=64) for h in range(2)]
-        steps = [(0, 0), (0, 1), (1, 1), (1, 0)]
-        for step, (h, u) in enumerate(steps):
+        steps = [(0, (0, 1)), (0, (2, 3)), (1, (3, 2)), (1, (0, 1))]
+        stores = {
+            (0, 0): (slice(0, 1), slice(0, HALF)),
+            (0, 2): (slice(1, 3), slice(0, HALF)),
+            (1, 3): (slice(3, 4), slice(0, NQ)),
+            (1, 1): (slice(0, 3), slice(HALF, NQ)),
+        }
+        for step, (h, pair) in enumerate(steps):
             cols = slice(h * HALF, (h + 1) * HALF)
-            y = y_all[:, 2 * u : 2 * u + 2, :]
-            for e in range(2):
-                r = 2 * u + e
+            places = slice(min(pair), max(pair) + 1)
+            for e, r in enumerate(pair):
                 part = slice(r * P, (r + 1) * P)
                 acc = psum.tile([P, HALF], F32, name="acc", tag="bank%d" % (2 * step + e))
                 nc.tensor.matmul_mx(
@@ -153,20 +158,16 @@ def tile_attend_plh_bgelu_topk_kernel(tc, qT, k_words, k_scales, nb, offs, out_0
                 width = PIECE if last else HALF
                 for c in range(0, HALF, width):
                     nc.scalar.activation(
-                        y[:, e, h * HALF + c : h * HALF + c + width], acc[:, c : c + width], GELU, bias=bias_cols[:, r : r + 1]
+                        y_all[:, r, h * HALF + c : h * HALF + c + width], acc[:, c : c + width], GELU, bias=bias_cols[:, r : r + 1]
                     )
-                if (h, r) == (0, 0):
-                    nc.sync.dma_start(y_rows[:, 0, cols], y_all[:, 0, cols])
-            places = slice(2 * u, 2 * u + 2)
-            if h == 1:
-                nc.sync.dma_start(y_rows[:, places, cols], y[:, :, cols])
-            elif u == 1:
-                nc.sync.dma_start(y_rows[:, 1:PACK, cols], y_all[:, 1:PACK, cols])
+                if (h, r) in stores:
+                    rows, span = stores[(h, r)]
+                    nc.sync.dma_start(y_rows[:, rows, span], y_all[:, rows, span])
             if step < len(steps) - 1:
-                weave(y[:, :, cols], y_wovens[h][:, :, places])
+                weave(y_all[:, places, cols], y_wovens[h][:, :, places])
             else:
                 for c in range(0, HALF, PIECE):
-                    weave(y[:, :, h * HALF + c : h * HALF + c + PIECE], y_wovens[h][:, c : c + PIECE, places])
+                    weave(y_all[:, places, h * HALF + c : h * HALF + c + PIECE], y_wovens[h][:, c : c + PIECE, places])
                 quantise_result(y_wovens[0][:], slice(0, HALF))
                 for c in range(0, HALF, PIECE):
                     quantise_result(y_wovens[h][:, c : c + PIECE, :], slice(h * HALF + c, h * HALF + c + PIECE))

@@ -23,7 +23,7 @@ PIECE = 64
 QUADS = 4
 BIAS_ROW = P - 1
 SCALE_ROW = P - 16
-EARLY = 512
+EARLY = 128
 
 FLOPS = 2 * SLOTS * 512 * NQ
 

from contextlib import ExitStack

import concourse.mybir as mybir
from concourse.masks import make_identity

F32 = mybir.dt.float32
BF16 = mybir.dt.bfloat16
I32 = mybir.dt.int32
U32 = mybir.dt.uint32
U16 = mybir.dt.uint16
U8 = mybir.dt.uint8
FP8X4 = mybir.dt.float8_e4m3fn_x4
GELU = mybir.ActivationFunctionType.Gelu_apprx_tanh
COPY = mybir.ActivationFunctionType.Copy

P = 128
PACK = 4
SLOTS = 512
POOL = 2048
NQ = 256
HALF = 128
PIECE = 64
QUADS = 4
BIAS_ROW = P - 1
SCALE_ROW = P - 16
EARLY = 128

FLOPS = 2 * SLOTS * 512 * NQ


def tile_attend_plh_bgelu_topk_kernel(tc, qT, k_words, k_scales, nb, offs, out_0, out_1, out_2):
    nc = tc.nc
    with ExitStack() as ctx:
        held = ctx.enter_context(tc.tile_pool(name="held", bufs=1))
        reused = ctx.enter_context(tc.tile_pool(name="reused", bufs=1))
        psum = ctx.enter_context(tc.psum_pool(name="psum", bufs=1))

        offsets = held.tile([P, SLOTS // 16], U16, name="offsets")
        nc.sync.dma_start(offsets[:], offs)

        scale_pool = held.tile([P, POOL], U8, name="scale_pool", align_bytes=64)
        nc.scalar.dma_start(scale_pool[SCALE_ROW : SCALE_ROW + 16, :].bitcast(I32), k_scales[0].bitcast(I32))
        bias_pool = held.tile([P, POOL], F32, name="bias_pool")
        nc.scalar.dma_start(bias_pool[BIAS_ROW:P, :], nb[0:1, :])
        ident = held.tile([P, P], F32, name="ident")
        nc.vector.memset(ident[:], 0.0)
        warm_out = held.tile([P, 1], F32, name="warm_out")
        nc.scalar.activation(warm_out[:], ident[:, 0:1], GELU)
        make_identity(nc, ident[:], nomemset=True)
        nc.vector.memset(scale_pool[0:SCALE_ROW, :].bitcast(I32), 0)
        scale_placed = held.tile([P, SLOTS], U8, name="scale_placed", tag="placed", align_bytes=64)
        nc.vector.memset(scale_placed[:].bitcast(I32), 0)
        nc.vector.memset(bias_pool[0:BIAS_ROW, :].bitcast(I32), 0)
        q_rows = qT[0].rearrange("(p j) q -> p j q", j=PACK)
        q_raw_first = reused.tile([P, PACK, HALF], F32, name="q_raw_first", offset=0, align_bytes=64)
        word_pool = held.tile([P, POOL], I32, name="word_pool")
        word_rows = k_words[0].rearrange("p n t -> p (n t)").bitcast(I32)

        nc.sync.dma_start(word_pool[:, 0:EARLY], word_rows[:, 0:EARLY])
        nc.sync.dma_start(word_pool[:, EARLY:POOL], word_rows[:, EARLY:POOL])
        nc.sync.dma_start(q_raw_first[:], q_rows[:, :, 0:HALF])
        q_raw_second = held.tile([P, PACK, HALF], F32, name="q_raw_second")
        nc.sync.dma_start(q_raw_second[:], q_rows[:, :, HALF:NQ])

        scale_listed = held.tile([P, SLOTS], U8, name="scale_listed", align_bytes=64)
        nc.vector.tensor_copy(scale_listed[:], scale_pool[:].indirect(offsets[:]))
        for quad in range(QUADS):
            first = SCALE_ROW + 4 * quad
            nc.sync.dma_start(
                scale_placed[32 * quad : 32 * quad + 4, :].bitcast(I32),
                scale_listed[first : first + 4, :].bitcast(I32),
            )
        q_raws = [q_raw_first, q_raw_second]
        bias_listed = held.tile([P, SLOTS], F32, name="bias_listed")
        nc.scalar.activation(bias_listed[:], bias_pool[:].indirect(offsets[:]), COPY)
        k_code = held.tile([P, SLOTS], I32, name="k_code", align_bytes=64)
        nc.vector.tensor_copy(
            k_code[:].bitcast(U32).rearrange("p (r s) -> p s r", r=PACK),
            word_pool[:].bitcast(U32).indirect(offsets[:]),
        )

        bias_turned = psum.tile([P, PACK, P], F32, name="bias_turned", tag="bank7")
        for r in range(PACK):
            nc.tensor.transpose(bias_turned[:, r, :], bias_listed[:, r:SLOTS:PACK], ident[:])


        y_code = held.tile([P, NQ], I32, name="y_code", align_bytes=64)
        y_rows = out_0.rearrange("(p r) q -> p r q", r=PACK)
        y_words = out_1[0].rearrange("p q u -> p (q u)").bitcast(I32)

        def weave(rows, woven):
            nc.vector.tensor_copy(
                woven.rearrange("p (c i) r -> p c r i", i=2),
                rows.rearrange("p r (c i) -> p c r i", i=2),
            )

        def quantise_result(woven, cols):
            nc.vector.quantize_mx(
                out=y_code[:, cols].bitcast(FP8X4),
                scales=y_scale[:, cols],
                in_=woven.rearrange("p c r -> p (c r)"),
            )

        q_wovens = [held.tile([P, HALF, PACK], BF16, name="q_woven%d" % h, align_bytes=64) for h in range(2)]
        q_codes = [held.tile([P, HALF], U32, name="q_code%d" % h, align_bytes=64) for h in range(2)]
        q_scales = [
            held.tile([P, HALF], U8, name="q_scale_first", align_bytes=64),
            held.tile([P, HALF], U8, name="q_scale_second", tag="placed", align_bytes=64),
        ]
        for h in range(NQ // HALF):
            nc.scalar.copy(
                q_wovens[h][:].rearrange("p (c i) j -> p c j i", i=4),
                q_raws[h][:].rearrange("p j (c i) -> p c j i", i=4),
            )

        bias_cols = reused.tile([P, PACK], F32, name="bias_cols", offset=SLOTS, align_bytes=64)
        nc.scalar.copy(bias_cols[:], bias_turned[:, :, BIAS_ROW])

        def quantise_queries(h):
            nc.vector.quantize_mx(
                out=q_codes[h][:].bitcast(FP8X4), scales=q_scales[h][:], in_=q_wovens[h][:].rearrange("p c j -> p (c j)")
            )

        quantise_queries(0)

        k_scale_dealt = reused.tile([P, SLOTS], U8, name="k_scale_dealt", offset=0, align_bytes=64)
        k_scale = [k_scale_dealt[:, r * P : (r + 1) * P] for r in range(PACK)]
        for r in range(PACK):
            nc.vector.tensor_copy(k_scale[r], scale_placed[:, r:SLOTS:PACK])
        quantise_queries(1)

        y_all = held.tile([P, PACK, NQ], F32, name="y_all")
        y_scale = reused.tile([P, NQ], U8, name="y_scale", offset=SLOTS, align_bytes=64)
        y_wovens = [held.tile([P, HALF, PACK], BF16, name="y_woven%d" % h, align_bytes=64) for h in range(2)]
        steps = [(0, (0, 1)), (0, (2, 3)), (1, (3, 2)), (1, (0, 1))]
        stores = {
            (0, 0): (slice(0, 1), slice(0, HALF)),
            (0, 2): (slice(1, 3), slice(0, HALF)),
            (1, 3): (slice(3, 4), slice(0, NQ)),
            (1, 1): (slice(0, 3), slice(HALF, NQ)),
        }
        for step, (h, pair) in enumerate(steps):
            cols = slice(h * HALF, (h + 1) * HALF)
            places = slice(min(pair), max(pair) + 1)
            for e, r in enumerate(pair):
                part = slice(r * P, (r + 1) * P)
                acc = psum.tile([P, HALF], F32, name="acc", tag="bank%d" % (2 * step + e))
                nc.tensor.matmul_mx(
                    out=acc[:],
                    lhsT=k_code[:, part].bitcast(FP8X4),
                    lhsT_scale=k_scale[r],
                    rhs=q_codes[h][:].bitcast(FP8X4),
                    rhs_scale=q_scales[h][:],
                    start=True,
                    stop=True,
                )
                last = step == len(steps) - 1 and e == 1
                width = PIECE if last else HALF
                for c in range(0, HALF, width):
                    nc.scalar.activation(
                        y_all[:, r, h * HALF + c : h * HALF + c + width], acc[:, c : c + width], GELU, bias=bias_cols[:, r : r + 1]
                    )
                if (h, r) in stores:
                    rows, span = stores[(h, r)]
                    nc.sync.dma_start(y_rows[:, rows, span], y_all[:, rows, span])
            if step < len(steps) - 1:
                weave(y_all[:, places, cols], y_wovens[h][:, :, places])
            else:
                for c in range(0, HALF, PIECE):
                    weave(y_all[:, places, h * HALF + c : h * HALF + c + PIECE], y_wovens[h][:, c : c + PIECE, places])
                quantise_result(y_wovens[0][:], slice(0, HALF))
                for c in range(0, HALF, PIECE):
                    quantise_result(y_wovens[h][:, c : c + PIECE, :], slice(h * HALF + c, h * HALF + c + PIECE))

        nc.sync.dma_start(y_words, y_code[:])
        for quad in range(QUADS):
            queue = nc.sync if quad % 2 else nc.scalar
            queue.dma_start(
                out_2[0, 4 * quad : 4 * quad + 4, :].bitcast(I32),
                y_scale[32 * quad : 32 * quad + 4, :].bitcast(I32),
            )
